import numpy as np
import ml_dtypes


def mxq(x, axis, fmt="e4m3"):
    dtype, down = {"e4m3": (ml_dtypes.float8_e4m3fn, 7), "e5m2": (ml_dtypes.float8_e5m2, 14)}[fmt]
    v = np.moveaxis(np.asarray(x, np.float32).astype(ml_dtypes.bfloat16).astype(np.float64), axis, -1)
    blocks = v.reshape(v.shape[:-1] + (-1, 32))
    amax = np.abs(blocks).max(-1, keepdims=True)
    byte = np.maximum(np.where(amax > 0, np.frexp(amax)[1] - 1 + 127, 0) - down, 1)
    scale = np.exp2(byte - 127.0)
    codes = (blocks / scale).astype(np.float32).astype(dtype).astype(np.float64)
    return np.moveaxis((codes * scale).reshape(v.shape), -1, axis)


WIDE = False


def mx_kscale(k):
    if not WIDE:
        return np.ones(k)
    levels = np.array([10, -10, 5, -5, 0])
    if k % 512:
        return np.exp2(np.random.permutation(np.resize(levels, k // 32))).repeat(32)
    a = np.empty((k // 512, 16))
    for p in range(k // 512):
        a[p, :8] = np.random.permutation(np.resize(levels, 8))
        for g in range(8):
            far = levels[np.abs(levels - a[p, g]) >= 10]
            a[p, g + 8] = far[np.random.randint(len(far))]
    return np.exp2(a.ravel()).repeat(32)


def f64(x):
    return np.asarray(x).astype(np.float64)


def striped8(idx):
    return np.asarray(idx).reshape(8, -1, 16).transpose(0, 2, 1).reshape(128, -1).astype(np.uint16)


def unstriped8(offs):
    return offs.reshape(8, 16, -1).transpose(0, 2, 1).reshape(8, -1).astype(np.int64)


def pick8(x, idx, run):
    r = np.arange(len(x))
    return x[r[:, None], idx[r % (8 * run) // run]]


E2M1 = np.array([0.0, 0.5, 1.0, 1.5, 2.0, 3.0, 4.0, 6.0, -0.0, -0.5, -1.0, -1.5, -2.0, -3.0, -4.0, -6.0])


def pack_weight(w, fmt):
    k, n = w.shape
    w = f64(np.asarray(w, np.float32).astype(ml_dtypes.bfloat16)).reshape(k // 32, 32, n)
    amax = np.abs(w).max(1)
    if fmt == "e4m3":
        byte = np.frexp(amax)[1] - 1 + 127 - 7
    else:
        mant, ex = np.frexp(amax / 6.0)
        byte = np.where(mant > 0.5, ex, ex - 1) + 127
    byte = np.clip(np.where(amax > 0, byte, 1), 1, 254)
    scaled = (w * np.exp2(127.0 - byte)[:, None, :]).reshape(k, n).astype(np.float32)
    by_word = np.ascontiguousarray(scaled.reshape(k // 512, 128, 4, n).transpose(0, 1, 3, 2))
    if fmt == "e4m3":
        words = by_word.astype(ml_dtypes.float8_e4m3fn).view(np.uint8)
    else:
        c = by_word.astype(ml_dtypes.float4_e2m1fn).view(np.uint8) & 0xF
        words = (c[..., 0::2] | (c[..., 1::2] << 4)).reshape(k // 512, 128, 2 * n)
    return np.ascontiguousarray(words), np.ascontiguousarray(byte.astype(np.uint8).reshape(k // 512, 16, n))


def unpack_weight(words, scales, fmt):
    g, _, n = scales.shape
    words = np.ascontiguousarray(words).reshape(g, 128, n, -1)
    if fmt == "e4m3":
        vals = words.view(ml_dtypes.float8_e4m3fn).astype(np.float64)
    else:
        nib = np.empty((g, 128, n, 4), np.uint8)
        nib[..., 0::2] = words & 0xF
        nib[..., 1::2] = words >> 4
        vals = E2M1[nib]
    vals = vals * np.repeat(np.exp2(scales.astype(np.float64) - 127.0), 8, axis=1)[..., None]
    return vals.transpose(0, 1, 3, 2).reshape(g * 512, n)


D, V, Q, I = 512, 2048, 128, 512


def setup_inputs():
    n = np.random.standard_normal
    idx = np.stack([np.random.permutation(V)[:I] for _ in range(8)])
    idx2 = np.stack([np.random.permutation(V)[:I] for _ in range(8)])
    fd = mx_kscale(D)
    vocp = pack_weight(n((D, V)) / fd[:, None], "e2m1")
    return {
        "hid": (n((D, Q)) * 0.8 / np.sqrt(D) * fd[:, None]).astype(np.float32),
        "voc_words": vocp[0],
        "voc_scales": vocp[1],
        "target": (np.random.uniform(0.0, 2.0, (Q, I))).astype(np.float32),
        "dhid": (n((D, Q)) * 1.0 / np.sqrt(D) * fd[:, None]).astype(np.float32),
        "base": (0.5 * n((Q, V))).astype(np.float32),
        "offs": striped8(idx),
        "offs2": striped8(idx2),
    }


def reference(hid, voc_words, voc_scales, target, dhid, base, offs, offs2):
    idx = unstriped8(offs)
    idx2 = unstriped8(offs2)
    vocu = unpack_weight(voc_words, voc_scales, "e2m1")
    hidq = mxq(f64(hid), 0, "e4m3")
    a = hidq.T @ vocu
    dhidq = mxq(f64(dhid), 0, "e4m3")
    ta = dhidq.T @ vocu
    p = np.exp(pick8(a, idx, 16))
    z = np.sum(p, axis=1, keepdims=True)
    b = np.exp(pick8(a, idx2, 16)) / z * 512.0
    db = f64(target) / (b + 1.0)
    dz = np.sum(db * 512.0 * np.exp(pick8(a, idx2, 16)) / np.square(z) * (-1.0), axis=1, keepdims=True)
    xp = pick8(ta, idx, 16) * p
    xz = np.sum(xp, axis=1, keepdims=True)
    xb = (pick8(ta, idx2, 16) * np.exp(pick8(a, idx2, 16)) - xz * np.exp(pick8(a, idx2, 16)) / z) / z * 512.0
    xdb = xb * f64(target) / np.square(b + 1.0) * (-1.0)
    xdz = np.sum((xdb * 512.0 * np.exp(pick8(a, idx2, 16)) + pick8(ta, idx2, 16) * np.exp(pick8(a, idx2, 16)) * db * 512.0 - xz * z * 2.0 * db * 512.0 * np.exp(pick8(a, idx2, 16)) / np.square(z)) / np.square(z) * (-1.0), axis=1, keepdims=True)
    xe1 = (xdb * 512.0 - xz * db * 512.0 / z) / z * np.exp(pick8(a, idx2, 16)) + pick8(ta, idx2, 16) * np.exp(pick8(a, idx2, 16)) * db * 512.0 / z
    xs1 = np.zeros((Q, V))
    xs1[np.arange(Q)[:, None], idx2[np.arange(Q) % 128 // 16]] = xe1
    xe2 = xdz * p + xp * dz
    xs2 = np.zeros((Q, V))
    xs2[np.arange(Q)[:, None], idx[np.arange(Q) % 128 // 16]] = xe2
    xda = xs1 + xs2
    y = xda + f64(base)
    return y

@@ -1,0 +1,173 @@
+import math
+from contextlib import ExitStack
+
+import concourse.mybir as mybir
+
+D, V, Q, I = 512, 2048, 128, 512
+FLOPS = 2 * 2 * D * Q * V
+
+F32 = mybir.dt.float32
+BF16 = mybir.dt.bfloat16
+I32 = mybir.dt.int32
+U32 = mybir.dt.uint32
+U16 = mybir.dt.uint16
+U8 = mybir.dt.uint8
+FP8X4 = mybir.dt.float8_e4m3fn_x4
+FP4X4 = mybir.dt.float4_e2m1fn_x4
+ALU = mybir.AluOpType
+ACT = mybir.ActivationFunctionType
+
+P = 128
+N = 512
+C = 512.0
+LN2 = math.log(2.0)
+OUT_CHUNKS = (256, 512, 512, 512, 256)
+
+
+def tile_attend_hvallowed_heads_kernel(tc, hid, voc_words, voc_scales, target, dhid, base, offs, offs2, out):
+    nc = tc.nc
+    with ExitStack() as ctx:
+        lists = ctx.enter_context(tc.tile_pool(name="lists", bufs=1))
+        sb = ctx.enter_context(tc.tile_pool(name="sb", bufs=1))
+        ps = ctx.enter_context(tc.psum_pool(name="ps", bufs=1))
+
+        def col(name):
+            return sb.tile([P, 1], F32, name=name)
+
+        def row(name, n=I):
+            return sb.tile([P, n], F32, name=name)
+
+        voc_sc = sb.tile([P, V], U8, name="voc_sc", align_bytes=64)
+        nc.vector.memset(voc_sc[:].bitcast(I32), 0)
+        warm_in = col("warm_in")
+        nc.vector.memset(warm_in[:], 0.0)
+        for quad in range(4):
+            nc.scalar.dma_start(
+                out=voc_sc[32 * quad : 32 * quad + 4, :].bitcast(I32),
+                in_=voc_scales[0, 4 * quad : 4 * quad + 4, :].bitcast(I32),
+            )
+        warm_out = col("warm_out")
+        nc.scalar.activation(warm_out[:], warm_in[:], ACT.Exp)
+
+        hid_raw = sb.tile([P, 4, Q], F32, name="hid_raw")
+        nc.sync.dma_start(out=hid_raw[:], in_=hid.rearrange("(p t) q -> p t q", t=4))
+        words = []
+        for h in range(2):
+            w = sb.tile([P, V], U8, name="words%d" % h, align_bytes=64)
+            nc.sync.dma_start(out=w[:].bitcast(I32), in_=voc_words[0, :, h * V : (h + 1) * V].bitcast(I32))
+            words.append(w)
+        dhid_raw = sb.tile([P, 4, Q], F32, name="dhid_raw")
+        nc.sync.dma_start(out=dhid_raw[:], in_=dhid.rearrange("(p t) q -> p t q", t=4))
+        list1 = lists.tile([P, I // 16], U16, name="list1")
+        nc.sync.dma_start(list1[:], offs)
+        list2 = lists.tile([P, I // 16], U16, name="list2")
+        nc.sync.dma_start(list2[:], offs2)
+        tgt = row("tgt")
+        nc.sync.dma_start(out=tgt[:], in_=target)
+        base_sb = row("base_sb", V)
+        nc.sync.dma_start(out=base_sb[:], in_=base)
+
+        xs1 = row("xs1", V)
+        nc.vector.memset(xs1[:], 0.0)
+
+        hid_bf = sb.tile([P, Q, 4], BF16, name="hid_bf", align_bytes=64)
+        dhid_bf = sb.tile([P, Q, 4], BF16, name="dhid_bf", tag="xs2", align_bytes=64)
+        nc.vector.tensor_copy(out=hid_bf[:], in_=hid_raw[:].rearrange("p t q -> p q t"))
+        nc.scalar.copy(out=dhid_bf[:], in_=dhid_raw[:].rearrange("p t q -> p q t"))
+        codes, planes = [], []
+        for name, src in (("hid", hid_bf), ("dhid", dhid_bf)):
+            cd = sb.tile([P, Q], U32, name=name + "_codes", align_bytes=64)
+            pl = sb.tile([P, Q], U8, name=name + "_plane", align_bytes=64)
+            nc.vector.quantize_mx(out=cd[:].bitcast(FP8X4), scales=pl[:], in_=src[:].rearrange("p q t -> p (q t)"))
+            codes.append(cd)
+            planes.append(pl)
+
+        xs2 = sb.tile([P, V], F32, name="xs2", tag="xs2", align_bytes=64)
+        nc.gpsimd.memset(xs2[:], 0.0)
+
+        a_sb = row("a_sb", V)
+        ta_sb = row("ta_sb", V)
+        for which, dst in enumerate((a_sb, ta_sb)):
+            for j in range(V // N):
+                bank = ps.tile([P, N], F32, name="bank%d" % (4 * which + j))
+                lo = (j % 2) * 2 * N
+                nc.tensor.matmul_mx(
+                    out=bank[:],
+                    lhsT=codes[which][:].bitcast(FP8X4),
+                    lhsT_scale=planes[which][:],
+                    rhs=words[j // 2][:, lo : lo + 2 * N].bitcast(FP4X4),
+                    rhs_scale=voc_sc[:, j * N : (j + 1) * N],
+                    start=True,
+                    stop=True,
+                )
+                if which == 0 and j % 2 == 1:
+                    nc.vector.tensor_copy(out=dst[:, j * N : (j + 1) * N], in_=bank[:])
+                else:
+                    nc.scalar.copy(out=dst[:, j * N : (j + 1) * N], in_=bank[:])
+
+        a1 = row("a1")
+        nc.vector.tensor_copy(a1[:], a_sb[:].indirect(list1[:]))
+        neg_max = col("neg_max")
+        nc.vector.tensor_reduce(out=neg_max[:], in_=a1[:], axis=mybir.AxisListType.X, op=ALU.max, negate=True)
+        a2 = row("a2")
+        nc.vector.tensor_copy(a2[:], a_sb[:].indirect(list2[:]))
+        p = row("p")
+        z = col("z")
+        nc.scalar.activation(p[:], a1[:], ACT.Exp, bias=neg_max[:], accum_out=z[:])
+        half_max = col("half_max")
+        nc.scalar.activation(half_max[:], neg_max[:], ACT.Copy, scale=-0.5, bias=0.25 - 0.5 * math.log(C))
+
+        bits = z[:].bitcast(U32)
+        kappa = LN2 / 2.0**23
+        e0, n1, q, k0, e1h, k1, beta = (col(n) for n in ("e0", "n1", "q", "k0", "e1h", "k1", "beta"))
+        nc.scalar.activation(e0[:], bits, ACT.Exp, scale=-kappa, bias=88.0)
+        nc.scalar.activation(n1[:], bits, ACT.Identity, scale=-kappa, bias=87.5)
+        nc.scalar.activation(q[:], e0[:], ACT.Square, scale=z[:], bias=-2.0)
+        nc.scalar.activation(k0[:], n1[:], ACT.Identity, scale=-0.5, bias=half_max[:])
+        nc.scalar.activation(e1h[:], q[:], ACT.Exp, scale=0.5, bias=n1[:])
+        nc.scalar.activation(k1[:], q[:], ACT.Identity, scale=-0.25, bias=k0[:])
+        q2 = col("q2")
+        nc.scalar.activation(q2[:], e1h[:], ACT.Square, scale=z[:], bias=-2.0)
+        nc.scalar.activation(beta[:], q2[:], ACT.Identity, scale=-0.25, bias=k1[:])
+        th = row("th")
+        nc.scalar.activation(th[:], a2[:], ACT.Tanh, scale=-0.5, bias=beta[:])
+
+        rz = col("rz")
+        nc.vector.reciprocal(rz[:], z[:])
+        xp = row("xp")
+        nc.vector.tensor_tensor(xp[:], ta_sb[:].indirect(list1[:]), p[:], ALU.mult)
+        t2q = row("t2q")
+        nc.vector.tensor_scalar(t2q[:], ta_sb[:].indirect(list2[:]), -0.25, 0.0, ALU.mult, ALU.add)
+        xq = row("xq")
+        xz4, m4, rzh, nrz, nm = (col(n) for n in ("xz4", "m4", "rzh", "nrz", "nm"))
+        nc.scalar.activation(xq[:], xp[:], ACT.Copy, scale=0.25, accum_out=xz4[:])
+        nc.scalar.activation(m4[:], xz4[:], ACT.Copy, scale=rz[:])
+        nc.scalar.activation(rzh[:], rz[:], ACT.Copy, scale=0.5)
+        nc.scalar.activation(nrz[:], rz[:], ACT.Copy, scale=-1.0)
+        nc.scalar.activation(nm[:], m4[:], ACT.Copy, scale=-4.0)
+
+        ts, y, xe1 = row("ts"), row("y"), row("xe1")
+        c1, x1 = col("c1"), col("x1")
+        nc.vector.scalar_tensor_tensor(ts[:], th[:], -1.0, tgt[:], ALU.add, ALU.mult, accum_out=c1[:])
+        nc.vector.scalar_tensor_tensor(y[:], th[:], 1.0, ts[:], ALU.add, ALU.mult)
+        nc.vector.scalar_tensor_tensor(xe1[:], t2q[:], m4[:], y[:], ALU.add, ALU.mult, accum_out=x1[:])
+        nc.vector.tensor_copy(xs1[:].indirect(list2[:]), xe1[:])
+
+        cb, mb, ca = col("cb"), col("mb"), col("ca")
+        u, v = row("u"), row("v")
+        nc.scalar.activation(cb[:], c1[:], ACT.Copy, scale=rzh[:])
+        nc.scalar.activation(mb[:], cb[:], ACT.Copy, scale=nm[:])
+        nc.scalar.activation(v[:], xp[:], ACT.Copy, scale=cb[:])
+        nc.scalar.activation(ca[:], x1[:], ACT.Identity, scale=nrz[:], bias=mb[:])
+        nc.scalar.activation(u[:], p[:], ACT.Copy, scale=ca[:])
+        nc.vector.tensor_tensor(xs2[:].indirect(list1[:]), u[:], v[:], ALU.add)
+
+        lo = 0
+        for j, width in enumerate(OUT_CHUNKS):
+            cols = slice(lo, lo + width)
+            part = row("part%d" % j, width)
+            res = row("res%d" % j, width)
+            nc.vector.tensor_tensor(part[:], xs2[:, cols], base_sb[:, cols], ALU.add)
+            nc.vector.tensor_tensor(res[:], part[:], xs1[:, cols], ALU.add)
+            nc.sync.dma_start(out=out[:, cols], in_=res[:])
+            lo = lo + width

@@ -40,22 +40,21 @@ def tile_attend_hvallowed_heads_kernel(tc, hid, voc_words, voc_scales, target, d
         voc_sc = sb.tile([P, V], U8, name="voc_sc", align_bytes=64)
         nc.vector.memset(voc_sc[:].bitcast(I32), 0)
         warm_in = col("warm_in")
-        nc.vector.memset(warm_in[:], 0.0)
-        for quad in range(4):
-            nc.scalar.dma_start(
-                out=voc_sc[32 * quad : 32 * quad + 4, :].bitcast(I32),
-                in_=voc_scales[0, 4 * quad : 4 * quad + 4, :].bitcast(I32),
-            )
+        nc.gpsimd.memset(warm_in[:], 0.0)
         warm_out = col("warm_out")
         nc.scalar.activation(warm_out[:], warm_in[:], ACT.Exp)
 
         hid_raw = sb.tile([P, 4, Q], F32, name="hid_raw")
         nc.sync.dma_start(out=hid_raw[:], in_=hid.rearrange("(p t) q -> p t q", t=4))
-        words = []
-        for h in range(2):
-            w = sb.tile([P, V], U8, name="words%d" % h, align_bytes=64)
-            nc.sync.dma_start(out=w[:].bitcast(I32), in_=voc_words[0, :, h * V : (h + 1) * V].bitcast(I32))
-            words.append(w)
+        words_first = sb.tile([P, 2 * N], U8, name="words_first", align_bytes=64)
+        nc.sync.dma_start(out=words_first[:].bitcast(I32), in_=voc_words[0, :, : 2 * N].bitcast(I32))
+        for quad in range(4):
+            nc.sync.dma_start(
+                out=voc_sc[32 * quad : 32 * quad + 4, :].bitcast(I32),
+                in_=voc_scales[0, 4 * quad : 4 * quad + 4, :].bitcast(I32),
+            )
+        words_rest = sb.tile([P, 2 * (V - N)], U8, name="words_rest", align_bytes=64)
+        nc.sync.dma_start(out=words_rest[:].bitcast(I32), in_=voc_words[0, :, 2 * N :].bitcast(I32))
         dhid_raw = sb.tile([P, 4, Q], F32, name="dhid_raw")
         nc.sync.dma_start(out=dhid_raw[:], in_=dhid.rearrange("(p t) q -> p t q", t=4))
         list1 = lists.tile([P, I // 16], U16, name="list1")
@@ -70,8 +69,8 @@ def tile_attend_hvallowed_heads_kernel(tc, hid, voc_words, voc_scales, target, d
         xs1 = row("xs1", V)
         nc.vector.memset(xs1[:], 0.0)
 
-        hid_bf = sb.tile([P, Q, 4], BF16, name="hid_bf", align_bytes=64)
-        dhid_bf = sb.tile([P, Q, 4], BF16, name="dhid_bf", tag="xs2", align_bytes=64)
+        hid_bf = sb.tile([P, Q, 4], BF16, name="hid_bf", tag="xs2", align_bytes=64)
+        dhid_bf = sb.tile([P, Q, 4], BF16, name="dhid_bf", align_bytes=64)
         nc.vector.tensor_copy(out=hid_bf[:], in_=hid_raw[:].rearrange("p t q -> p q t"))
         nc.scalar.copy(out=dhid_bf[:], in_=dhid_raw[:].rearrange("p t q -> p q t"))
         codes, planes = [], []
@@ -87,23 +86,29 @@ def tile_attend_hvallowed_heads_kernel(tc, hid, voc_words, voc_scales, target, d
 
         a_sb = row("a_sb", V)
         ta_sb = row("ta_sb", V)
-        for which, dst in enumerate((a_sb, ta_sb)):
-            for j in range(V // N):
-                bank = ps.tile([P, N], F32, name="bank%d" % (4 * which + j))
-                lo = (j % 2) * 2 * N
-                nc.tensor.matmul_mx(
-                    out=bank[:],
-                    lhsT=codes[which][:].bitcast(FP8X4),
-                    lhsT_scale=planes[which][:],
-                    rhs=words[j // 2][:, lo : lo + 2 * N].bitcast(FP4X4),
-                    rhs_scale=voc_sc[:, j * N : (j + 1) * N],
-                    start=True,
-                    stop=True,
-                )
-                if which == 0 and j % 2 == 1:
-                    nc.vector.tensor_copy(out=dst[:, j * N : (j + 1) * N], in_=bank[:])
-                else:
-                    nc.scalar.copy(out=dst[:, j * N : (j + 1) * N], in_=bank[:])
+        def voc_cols(lo, width):
+            if lo < N:
+                return words_first[:, 2 * lo : 2 * (lo + width)]
+            return words_rest[:, 2 * (lo - N) : 2 * (lo - N + width)]
+
+        passes = [(0, 0, N), (0, N, N), (0, 2 * N, N), (0, 3 * N, N // 2), (0, 3 * N + N // 2, N // 2)]
+        passes = passes + [(1, j * N, N) for j in range(V // N)]
+        for j, (which, lo, width) in enumerate(passes):
+            dst = (a_sb, ta_sb)[which]
+            bank = ps.tile([P, N], F32, name="bank%d" % (j % 8))
+            nc.tensor.matmul_mx(
+                out=bank[:, :width],
+                lhsT=codes[which][:].bitcast(FP8X4),
+                lhsT_scale=planes[which][:],
+                rhs=voc_cols(lo, width).bitcast(FP4X4),
+                rhs_scale=voc_sc[:, lo : lo + width],
+                start=True,
+                stop=True,
+            )
+            if which == 0 and j % 2 == 0:
+                nc.vector.tensor_copy(out=dst[:, lo : lo + width], in_=bank[:, :width])
+            else:
+                nc.scalar.copy(out=dst[:, lo : lo + width], in_=bank[:, :width])
 
         a1 = row("a1")
         nc.vector.tensor_copy(a1[:], a_sb[:].indirect(list1[:]))
@@ -129,8 +134,10 @@ def tile_attend_hvallowed_heads_kernel(tc, hid, voc_words, voc_scales, target, d
         q2 = col("q2")
         nc.scalar.activation(q2[:], e1h[:], ACT.Square, scale=z[:], bias=-2.0)
         nc.scalar.activation(beta[:], q2[:], ACT.Identity, scale=-0.25, bias=k1[:])
-        th = row("th")
-        nc.scalar.activation(th[:], a2[:], ACT.Tanh, scale=-0.5, bias=beta[:])
+        halves = (slice(0, I // 2), slice(I // 2, I))
+        th = [row("th%d" % h, I // 2) for h in range(2)]
+        for h in range(2):
+            nc.scalar.activation(th[h][:], a2[:, halves[h]], ACT.Tanh, scale=-0.5, bias=beta[:])
 
         rz = col("rz")
         nc.vector.reciprocal(rz[:], z[:])
@@ -138,36 +145,62 @@ def tile_attend_hvallowed_heads_kernel(tc, hid, voc_words, voc_scales, target, d
         nc.vector.tensor_tensor(xp[:], ta_sb[:].indirect(list1[:]), p[:], ALU.mult)
         t2q = row("t2q")
         nc.vector.tensor_scalar(t2q[:], ta_sb[:].indirect(list2[:]), -0.25, 0.0, ALU.mult, ALU.add)
-        xq = row("xq")
-        xz4, m4, rzh, nrz, nm = (col(n) for n in ("xz4", "m4", "rzh", "nrz", "nm"))
+        xq = sb.tile([P, I], F32, name="xq", tag="a2")
+        rzh = sb.tile([P, 1], F32, name="rzh", tag="q2")
+        nrz = sb.tile([P, 1], F32, name="nrz", tag="k1")
+        xz4, m4, nm = (col(n) for n in ("xz4", "m4", "nm"))
         nc.scalar.activation(xq[:], xp[:], ACT.Copy, scale=0.25, accum_out=xz4[:])
         nc.scalar.activation(m4[:], xz4[:], ACT.Copy, scale=rz[:])
         nc.scalar.activation(rzh[:], rz[:], ACT.Copy, scale=0.5)
         nc.scalar.activation(nrz[:], rz[:], ACT.Copy, scale=-1.0)
         nc.scalar.activation(nm[:], m4[:], ACT.Copy, scale=-4.0)
 
-        ts, y, xe1 = row("ts"), row("y"), row("xe1")
-        c1, x1 = col("c1"), col("x1")
-        nc.vector.scalar_tensor_tensor(ts[:], th[:], -1.0, tgt[:], ALU.add, ALU.mult, accum_out=c1[:])
-        nc.vector.scalar_tensor_tensor(y[:], th[:], 1.0, ts[:], ALU.add, ALU.mult)
-        nc.vector.scalar_tensor_tensor(xe1[:], t2q[:], m4[:], y[:], ALU.add, ALU.mult, accum_out=x1[:])
+        ts = [row("ts%d" % h, I // 2) for h in range(2)]
+        y = [row("y%d" % h, I // 2) for h in range(2)]
+        xe1 = row("xe1")
+        c1 = [col("c1_%d" % h) for h in range(2)]
+        x1 = [col("x1_%d" % h) for h in range(2)]
+        for h in range(2):
+            nc.vector.scalar_tensor_tensor(ts[h][:], th[h][:], -1.0, tgt[:, halves[h]], ALU.add, ALU.mult, accum_out=c1[h][:])
+        for h in range(2):
+            nc.vector.scalar_tensor_tensor(y[h][:], th[h][:], 1.0, ts[h][:], ALU.add, ALU.mult)
+        for h in range(2):
+            nc.vector.scalar_tensor_tensor(
+                xe1[:, halves[h]], t2q[:, halves[h]], m4[:], y[h][:], ALU.add, ALU.mult, accum_out=x1[h][:]
+            )
         nc.vector.tensor_copy(xs1[:].indirect(list2[:]), xe1[:])
 
-        cb, mb, ca = col("cb"), col("mb"), col("ca")
-        u, v = row("u"), row("v")
-        nc.scalar.activation(cb[:], c1[:], ACT.Copy, scale=rzh[:])
+        c1s, cb, mb, ca0, ca = (col(n) for n in ("c1s", "cb", "mb", "ca0", "ca"))
+        v = row("v")
+        nc.scalar.activation(c1s[:], c1[0][:], ACT.Identity, bias=c1[1][:])
+        nc.scalar.activation(cb[:], c1s[:], ACT.Copy, scale=rzh[:])
         nc.scalar.activation(mb[:], cb[:], ACT.Copy, scale=nm[:])
         nc.scalar.activation(v[:], xp[:], ACT.Copy, scale=cb[:])
-        nc.scalar.activation(ca[:], x1[:], ACT.Identity, scale=nrz[:], bias=mb[:])
-        nc.scalar.activation(u[:], p[:], ACT.Copy, scale=ca[:])
-        nc.vector.tensor_tensor(xs2[:].indirect(list1[:]), u[:], v[:], ALU.add)
+        nc.scalar.activation(ca0[:], x1[0][:], ACT.Identity, scale=nrz[:], bias=mb[:])
+        nc.scalar.activation(ca[:], x1[1][:], ACT.Identity, scale=nrz[:], bias=ca0[:])
+        xe2 = row("xe2")
+        for h in range(2):
+            u = row("u%d" % h, I // 2)
+            nc.scalar.activation(u[:], p[:, halves[h]], ACT.Copy, scale=ca[:])
+            nc.gpsimd.tensor_tensor(xe2[:, halves[h]], u[:], v[:, halves[h]], ALU.add)
+        nc.vector.tensor_copy(xs2[:].indirect(list1[:]), xe2[:])
 
-        lo = 0
-        for j, width in enumerate(OUT_CHUNKS):
-            cols = slice(lo, lo + width)
-            part = row("part%d" % j, width)
-            res = row("res%d" % j, width)
-            nc.vector.tensor_tensor(part[:], xs2[:, cols], base_sb[:, cols], ALU.add)
-            nc.vector.tensor_tensor(res[:], part[:], xs1[:, cols], ALU.add)
-            nc.sync.dma_start(out=out[:, cols], in_=res[:])
-            lo = lo + width
+        edges = [sum(OUT_CHUNKS[:j]) for j in range(len(OUT_CHUNKS) + 1)]
+        chunks = [slice(edges[j], edges[j + 1]) for j in range(len(OUT_CHUNKS))]
+        early = sb.tile([P, edges[3]], F32, name="early", tag="v")
+        parts = [early[:, chunks[j]] for j in range(3)] + [row("part%d" % j, OUT_CHUNKS[j])[:] for j in (3, 4)]
+        for j in range(3):
+            nc.gpsimd.tensor_tensor(parts[j], xs1[:, chunks[j]], base_sb[:, chunks[j]], ALU.add)
+
+        def finish(j, other):
+            res = row("res%d" % j, OUT_CHUNKS[j])
+            nc.vector.tensor_tensor(res[:], parts[j], other[:, chunks[j]], ALU.add)
+            nc.sync.dma_start(out=out[:, chunks[j]], in_=res[:])
+
+        finish(0, xs2)
+        finish(1, xs2)
+        nc.vector.tensor_tensor(parts[3], xs2[:, chunks[3]], base_sb[:, chunks[3]], ALU.add)
+        finish(2, xs2)
+        nc.vector.tensor_tensor(parts[4], xs2[:, chunks[4]], base_sb[:, chunks[4]], ALU.add)
+        finish(3, xs1)
+        finish(4, xs1)

import math
from contextlib import ExitStack

import concourse.mybir as mybir

D, V, Q, I = 512, 2048, 128, 512
FLOPS = 2 * 2 * D * Q * V

F32 = mybir.dt.float32
BF16 = mybir.dt.bfloat16
I32 = mybir.dt.int32
U32 = mybir.dt.uint32
U16 = mybir.dt.uint16
U8 = mybir.dt.uint8
FP8X4 = mybir.dt.float8_e4m3fn_x4
FP4X4 = mybir.dt.float4_e2m1fn_x4
ALU = mybir.AluOpType
ACT = mybir.ActivationFunctionType

P = 128
N = 512
C = 512.0
LN2 = math.log(2.0)
OUT_CHUNKS = (256, 512, 512, 512, 256)


def tile_attend_hvallowed_heads_kernel(tc, hid, voc_words, voc_scales, target, dhid, base, offs, offs2, out):
    nc = tc.nc
    with ExitStack() as ctx:
        lists = ctx.enter_context(tc.tile_pool(name="lists", bufs=1))
        sb = ctx.enter_context(tc.tile_pool(name="sb", bufs=1))
        ps = ctx.enter_context(tc.psum_pool(name="ps", bufs=1))

        def col(name):
            return sb.tile([P, 1], F32, name=name)

        def row(name, n=I):
            return sb.tile([P, n], F32, name=name)

        voc_sc = sb.tile([P, V], U8, name="voc_sc", align_bytes=64)
        nc.vector.memset(voc_sc[:].bitcast(I32), 0)
        warm_in = col("warm_in")
        nc.gpsimd.memset(warm_in[:], 0.0)
        warm_out = col("warm_out")
        nc.scalar.activation(warm_out[:], warm_in[:], ACT.Exp)

        hid_raw = sb.tile([P, 4, Q], F32, name="hid_raw")
        nc.sync.dma_start(out=hid_raw[:], in_=hid.rearrange("(p t) q -> p t q", t=4))
        words_first = sb.tile([P, 2 * N], U8, name="words_first", align_bytes=64)
        nc.sync.dma_start(out=words_first[:].bitcast(I32), in_=voc_words[0, :, : 2 * N].bitcast(I32))
        for quad in range(4):
            nc.sync.dma_start(
                out=voc_sc[32 * quad : 32 * quad + 4, :].bitcast(I32),
                in_=voc_scales[0, 4 * quad : 4 * quad + 4, :].bitcast(I32),
            )
        words_rest = sb.tile([P, 2 * (V - N)], U8, name="words_rest", align_bytes=64)
        nc.sync.dma_start(out=words_rest[:].bitcast(I32), in_=voc_words[0, :, 2 * N :].bitcast(I32))
        dhid_raw = sb.tile([P, 4, Q], F32, name="dhid_raw")
        nc.sync.dma_start(out=dhid_raw[:], in_=dhid.rearrange("(p t) q -> p t q", t=4))
        list1 = lists.tile([P, I // 16], U16, name="list1")
        nc.sync.dma_start(list1[:], offs)
        list2 = lists.tile([P, I // 16], U16, name="list2")
        nc.sync.dma_start(list2[:], offs2)
        tgt = row("tgt")
        nc.sync.dma_start(out=tgt[:], in_=target)
        base_sb = row("base_sb", V)
        nc.sync.dma_start(out=base_sb[:], in_=base)

        xs1 = row("xs1", V)
        nc.vector.memset(xs1[:], 0.0)

        hid_bf = sb.tile([P, Q, 4], BF16, name="hid_bf", tag="xs2", align_bytes=64)
        dhid_bf = sb.tile([P, Q, 4], BF16, name="dhid_bf", align_bytes=64)
        nc.vector.tensor_copy(out=hid_bf[:], in_=hid_raw[:].rearrange("p t q -> p q t"))
        nc.scalar.copy(out=dhid_bf[:], in_=dhid_raw[:].rearrange("p t q -> p q t"))
        codes, planes = [], []
        for name, src in (("hid", hid_bf), ("dhid", dhid_bf)):
            cd = sb.tile([P, Q], U32, name=name + "_codes", align_bytes=64)
            pl = sb.tile([P, Q], U8, name=name + "_plane", align_bytes=64)
            nc.vector.quantize_mx(out=cd[:].bitcast(FP8X4), scales=pl[:], in_=src[:].rearrange("p q t -> p (q t)"))
            codes.append(cd)
            planes.append(pl)

        xs2 = sb.tile([P, V], F32, name="xs2", tag="xs2", align_bytes=64)
        nc.gpsimd.memset(xs2[:], 0.0)

        a_sb = row("a_sb", V)
        ta_sb = row("ta_sb", V)
        def voc_cols(lo, width):
            if lo < N:
                return words_first[:, 2 * lo : 2 * (lo + width)]
            return words_rest[:, 2 * (lo - N) : 2 * (lo - N + width)]

        passes = [(0, 0, N), (0, N, N), (0, 2 * N, N), (0, 3 * N, N // 2), (0, 3 * N + N // 2, N // 2)]
        passes = passes + [(1, j * N, N) for j in range(V // N)]
        for j, (which, lo, width) in enumerate(passes):
            dst = (a_sb, ta_sb)[which]
            bank = ps.tile([P, N], F32, name="bank%d" % (j % 8))
            nc.tensor.matmul_mx(
                out=bank[:, :width],
                lhsT=codes[which][:].bitcast(FP8X4),
                lhsT_scale=planes[which][:],
                rhs=voc_cols(lo, width).bitcast(FP4X4),
                rhs_scale=voc_sc[:, lo : lo + width],
                start=True,
                stop=True,
            )
            if which == 0 and j % 2 == 0:
                nc.vector.tensor_copy(out=dst[:, lo : lo + width], in_=bank[:, :width])
            else:
                nc.scalar.copy(out=dst[:, lo : lo + width], in_=bank[:, :width])

        a1 = row("a1")
        nc.vector.tensor_copy(a1[:], a_sb[:].indirect(list1[:]))
        neg_max = col("neg_max")
        nc.vector.tensor_reduce(out=neg_max[:], in_=a1[:], axis=mybir.AxisListType.X, op=ALU.max, negate=True)
        a2 = row("a2")
        nc.vector.tensor_copy(a2[:], a_sb[:].indirect(list2[:]))
        p = row("p")
        z = col("z")
        nc.scalar.activation(p[:], a1[:], ACT.Exp, bias=neg_max[:], accum_out=z[:])
        half_max = col("half_max")
        nc.scalar.activation(half_max[:], neg_max[:], ACT.Copy, scale=-0.5, bias=0.25 - 0.5 * math.log(C))

        bits = z[:].bitcast(U32)
        kappa = LN2 / 2.0**23
        e0, n1, q, k0, e1h, k1, beta = (col(n) for n in ("e0", "n1", "q", "k0", "e1h", "k1", "beta"))
        nc.scalar.activation(e0[:], bits, ACT.Exp, scale=-kappa, bias=88.0)
        nc.scalar.activation(n1[:], bits, ACT.Identity, scale=-kappa, bias=87.5)
        nc.scalar.activation(q[:], e0[:], ACT.Square, scale=z[:], bias=-2.0)
        nc.scalar.activation(k0[:], n1[:], ACT.Identity, scale=-0.5, bias=half_max[:])
        nc.scalar.activation(e1h[:], q[:], ACT.Exp, scale=0.5, bias=n1[:])
        nc.scalar.activation(k1[:], q[:], ACT.Identity, scale=-0.25, bias=k0[:])
        q2 = col("q2")
        nc.scalar.activation(q2[:], e1h[:], ACT.Square, scale=z[:], bias=-2.0)
        nc.scalar.activation(beta[:], q2[:], ACT.Identity, scale=-0.25, bias=k1[:])
        halves = (slice(0, I // 2), slice(I // 2, I))
        th = [row("th%d" % h, I // 2) for h in range(2)]
        for h in range(2):
            nc.scalar.activation(th[h][:], a2[:, halves[h]], ACT.Tanh, scale=-0.5, bias=beta[:])

        rz = col("rz")
        nc.vector.reciprocal(rz[:], z[:])
        xp = row("xp")
        nc.vector.tensor_tensor(xp[:], ta_sb[:].indirect(list1[:]), p[:], ALU.mult)
        t2q = row("t2q")
        nc.vector.tensor_scalar(t2q[:], ta_sb[:].indirect(list2[:]), -0.25, 0.0, ALU.mult, ALU.add)
        xq = sb.tile([P, I], F32, name="xq", tag="a2")
        rzh = sb.tile([P, 1], F32, name="rzh", tag="q2")
        nrz = sb.tile([P, 1], F32, name="nrz", tag="k1")
        xz4, m4, nm = (col(n) for n in ("xz4", "m4", "nm"))
        nc.scalar.activation(xq[:], xp[:], ACT.Copy, scale=0.25, accum_out=xz4[:])
        nc.scalar.activation(m4[:], xz4[:], ACT.Copy, scale=rz[:])
        nc.scalar.activation(rzh[:], rz[:], ACT.Copy, scale=0.5)
        nc.scalar.activation(nrz[:], rz[:], ACT.Copy, scale=-1.0)
        nc.scalar.activation(nm[:], m4[:], ACT.Copy, scale=-4.0)

        ts = [row("ts%d" % h, I // 2) for h in range(2)]
        y = [row("y%d" % h, I // 2) for h in range(2)]
        xe1 = row("xe1")
        c1 = [col("c1_%d" % h) for h in range(2)]
        x1 = [col("x1_%d" % h) for h in range(2)]
        for h in range(2):
            nc.vector.scalar_tensor_tensor(ts[h][:], th[h][:], -1.0, tgt[:, halves[h]], ALU.add, ALU.mult, accum_out=c1[h][:])
        for h in range(2):
            nc.vector.scalar_tensor_tensor(y[h][:], th[h][:], 1.0, ts[h][:], ALU.add, ALU.mult)
        for h in range(2):
            nc.vector.scalar_tensor_tensor(
                xe1[:, halves[h]], t2q[:, halves[h]], m4[:], y[h][:], ALU.add, ALU.mult, accum_out=x1[h][:]
            )
        nc.vector.tensor_copy(xs1[:].indirect(list2[:]), xe1[:])

        c1s, cb, mb, ca0, ca = (col(n) for n in ("c1s", "cb", "mb", "ca0", "ca"))
        v = row("v")
        nc.scalar.activation(c1s[:], c1[0][:], ACT.Identity, bias=c1[1][:])
        nc.scalar.activation(cb[:], c1s[:], ACT.Copy, scale=rzh[:])
        nc.scalar.activation(mb[:], cb[:], ACT.Copy, scale=nm[:])
        nc.scalar.activation(v[:], xp[:], ACT.Copy, scale=cb[:])
        nc.scalar.activation(ca0[:], x1[0][:], ACT.Identity, scale=nrz[:], bias=mb[:])
        nc.scalar.activation(ca[:], x1[1][:], ACT.Identity, scale=nrz[:], bias=ca0[:])
        xe2 = row("xe2")
        for h in range(2):
            u = row("u%d" % h, I // 2)
            nc.scalar.activation(u[:], p[:, halves[h]], ACT.Copy, scale=ca[:])
            nc.gpsimd.tensor_tensor(xe2[:, halves[h]], u[:], v[:, halves[h]], ALU.add)
        nc.vector.tensor_copy(xs2[:].indirect(list1[:]), xe2[:])

        edges = [sum(OUT_CHUNKS[:j]) for j in range(len(OUT_CHUNKS) + 1)]
        chunks = [slice(edges[j], edges[j + 1]) for j in range(len(OUT_CHUNKS))]
        early = sb.tile([P, edges[3]], F32, name="early", tag="v")
        parts = [early[:, chunks[j]] for j in range(3)] + [row("part%d" % j, OUT_CHUNKS[j])[:] for j in (3, 4)]
        for j in range(3):
            nc.gpsimd.tensor_tensor(parts[j], xs1[:, chunks[j]], base_sb[:, chunks[j]], ALU.add)

        def finish(j, other):
            res = row("res%d" % j, OUT_CHUNKS[j])
            nc.vector.tensor_tensor(res[:], parts[j], other[:, chunks[j]], ALU.add)
            nc.sync.dma_start(out=out[:, chunks[j]], in_=res[:])

        finish(0, xs2)
        finish(1, xs2)
        nc.vector.tensor_tensor(parts[3], xs2[:, chunks[3]], base_sb[:, chunks[3]], ALU.add)
        finish(2, xs2)
        nc.vector.tensor_tensor(parts[4], xs2[:, chunks[4]], base_sb[:, chunks[4]], ALU.add)
        finish(3, xs1)
        finish(4, xs1)
